import numpy as np
import ml_dtypes


def mxq(x, axis, fmt="e4m3"):
    dtype, down = {"e4m3": (ml_dtypes.float8_e4m3fn, 7), "e5m2": (ml_dtypes.float8_e5m2, 14)}[fmt]
    v = np.moveaxis(np.asarray(x, np.float32).astype(ml_dtypes.bfloat16).astype(np.float64), axis, -1)
    blocks = v.reshape(v.shape[:-1] + (-1, 32))
    amax = np.abs(blocks).max(-1, keepdims=True)
    byte = np.maximum(np.where(amax > 0, np.frexp(amax)[1] - 1 + 127, 0) - down, 1)
    scale = np.exp2(byte - 127.0)
    codes = (blocks / scale).astype(np.float32).astype(dtype).astype(np.float64)
    return np.moveaxis((codes * scale).reshape(v.shape), -1, axis)


WIDE = False


def mx_kscale(k):
    if not WIDE:
        return np.ones(k)
    levels = np.array([30, -30])
    if k % 512:
        return np.exp2(np.random.permutation(np.resize(levels, k // 32))).repeat(32)
    a = np.empty((k // 512, 16))
    for p in range(k // 512):
        a[p, :8] = np.random.permutation(np.resize(levels, 8))
        for g in range(8):
            far = levels[np.abs(levels - a[p, g]) >= 10]
            a[p, g + 8] = far[np.random.randint(len(far))]
    return np.exp2(a.ravel()).repeat(32)


def f64(x):
    return np.asarray(x).astype(np.float64)


def striped(idx):
    return np.tile(np.asarray(idx).reshape(-1, 16).T, (8, 1)).astype(np.uint16)


def unstriped(offs):
    return offs[:16].T.reshape(-1).astype(np.int64)


E2M1 = np.array([0.0, 0.5, 1.0, 1.5, 2.0, 3.0, 4.0, 6.0, -0.0, -0.5, -1.0, -1.5, -2.0, -3.0, -4.0, -6.0])


def pack_weight(w, fmt):
    k, n = w.shape
    w = f64(np.asarray(w, np.float32).astype(ml_dtypes.bfloat16)).reshape(k // 32, 32, n)
    amax = np.abs(w).max(1)
    if fmt in ("e4m3", "e5m2"):
        byte = np.frexp(amax)[1] - 1 + 127 - (7 if fmt == "e4m3" else 14)
    else:
        mant, ex = np.frexp(amax / 6.0)
        byte = np.where(mant > 0.5, ex, ex - 1) + 127
    byte = np.clip(np.where(amax > 0, byte, 1), 1, 254)
    scaled = (w * np.exp2(127.0 - byte)[:, None, :]).reshape(k, n).astype(np.float32)
    by_word = np.ascontiguousarray(scaled.reshape(k // 512, 128, 4, n).transpose(0, 1, 3, 2))
    if fmt in ("e4m3", "e5m2"):
        words = by_word.astype(ml_dtypes.float8_e4m3fn if fmt == "e4m3" else ml_dtypes.float8_e5m2).view(np.uint8)
    else:
        c = by_word.astype(ml_dtypes.float4_e2m1fn).view(np.uint8) & 0xF
        words = (c[..., 0::2] | (c[..., 1::2] << 4)).reshape(k // 512, 128, 2 * n)
    return np.ascontiguousarray(words), np.ascontiguousarray(byte.astype(np.uint8).reshape(k // 512, 16, n))


def unpack_weight(words, scales, fmt):
    g, _, n = scales.shape
    words = np.ascontiguousarray(words).reshape(g, 128, n, -1)
    if fmt in ("e4m3", "e5m2"):
        vals = words.view(ml_dtypes.float8_e4m3fn if fmt == "e4m3" else ml_dtypes.float8_e5m2).astype(np.float64)
    else:
        nib = np.empty((g, 128, n, 4), np.uint8)
        nib[..., 0::2] = words & 0xF
        nib[..., 1::2] = words >> 4
        vals = E2M1[nib]
    vals = vals * np.repeat(np.exp2(scales.astype(np.float64) - 127.0), 8, axis=1)[..., None]
    return vals.transpose(0, 1, 3, 2).reshape(g * 512, n)


K, T, J, R, V, N = 1024, 1024, 256, 512, 512, 256


def setup_inputs():
    n = np.random.standard_normal
    idx = np.random.permutation(T)[:J]
    idx2 = np.random.permutation(V)[:J]
    fk = mx_kscale(K)
    fr = mx_kscale(R)
    xtp = pack_weight(n((K, T)) / fk[:, None], "e2m1")
    wp = pack_weight(n((K, R)) * 1 / np.sqrt(K) * fk[:, None] * fr, "e2m1")
    wbp = pack_weight(n((R, N)) * 1 / np.sqrt(R) / fr[:, None], "e5m2")
    return {
        "xt_words": xtp[0],
        "xt_scales": xtp[1],
        "w_words": wp[0],
        "w_scales": wp[1],
        "tb": (n((R, V)) * 0.7 * fr[:, None]).astype(np.float32),
        "wb_words": wbp[0],
        "wb_scales": wbp[1],
        "bi": (np.random.uniform(-0.5, 0.5, (1, N))).astype(np.float32),
        "offs": striped(idx),
        "offs2": striped(idx2),
    }


def reference(xt_words, xt_scales, w_words, w_scales, tb, wb_words, wb_scales, bi, offs, offs2):
    idx = unstriped(offs)
    idx2 = unstriped(offs2)
    xtu = unpack_weight(xt_words, xt_scales, "e2m1")
    wu = unpack_weight(w_words, w_scales, "e2m1")
    wbu = unpack_weight(wb_words, wb_scales, "e5m2")
    xtidxg = xtu[:, idx]
    a = wu.T @ xtidxg
    hid = np.maximum(a - f64(tb)[:, idx2], 0.0)
    hidq = mxq(hid, 0, "e5m2")
    p = hidq.T @ wbu
    ea = np.exp(0.7 * p + f64(bi))
    y = 256.0 * ea / np.sum(ea, axis=1, keepdims=True)
    return y

@@ -1,0 +1,158 @@
+from contextlib import ExitStack
+
+import concourse.mybir as mybir
+
+K, T, J, R, V, N = 1024, 1024, 256, 512, 512, 256
+FLOPS = 2 * K * R * J + 2 * R * J * N
+
+F32 = mybir.dt.float32
+BF16 = mybir.dt.bfloat16
+I32 = mybir.dt.int32
+U32 = mybir.dt.uint32
+U16 = mybir.dt.uint16
+U8 = mybir.dt.uint8
+FP4X4 = mybir.dt.float4_e2m1fn_x4
+E5M2X4 = mybir.dt.float8_e5m2_x4
+ALU = mybir.AluOpType
+ACT = mybir.ActivationFunctionType
+AXIS = mybir.AxisListType
+
+P = 128
+PACK = 4
+PASSES = K // (P * PACK)
+QUADS = 4
+HALVES = J // P
+LIST_COLS = P // 16
+
+
+def load_scale_rows(queue, plane, scales):
+    for q in range(QUADS):
+        queue.dma_start(
+            out=plane[32 * q : 32 * q + 4, :, :].bitcast(I32),
+            in_=scales[:, 4 * q : 4 * q + 4, :].rearrange("z r c -> r z c").bitcast(I32),
+        )
+
+
+def tile_list_picked_overtable_rowshares_kernel(
+    tc, xt_words, xt_scales, w_words, w_scales, tb, wb_words, wb_scales, bi, offs, offs2, out
+):
+    nc = tc.nc
+    with ExitStack() as ctx:
+        lists = ctx.enter_context(tc.tile_pool(name="lists", bufs=1))
+        sb = ctx.enter_context(tc.tile_pool(name="sb", bufs=1))
+        psum = ctx.enter_context(tc.psum_pool(name="psum", bufs=1))
+
+        tok_list = lists.tile([P, J // 16], U16, name="tok_list")
+        tab_list = lists.tile([P, J // 16], U16, name="tab_list")
+
+        w_raw = sb.tile([P, PASSES, R], U16, name="w_raw", align_bytes=64)
+        ws_raw = sb.tile([P, PASSES, R], U8, name="ws_raw", align_bytes=64)
+        x_raw = [sb.tile([P, T], U16, name="x_raw%d" % z, align_bytes=64) for z in range(PASSES)]
+        xs_raw = sb.tile([P, PASSES, T], U8, name="xs_raw", align_bytes=64)
+        tab = [sb.tile([P, 2, V], F32, name="tab%d" % u, align_bytes=64) for u in range(PACK // 2)]
+        wb_codes = sb.tile([P, N], U32, name="wb_codes", align_bytes=64)
+        wb_plane = sb.tile([P, 1, N], U8, name="wb_plane", align_bytes=64)
+        bias = sb.tile([P, N], F32, name="bias", align_bytes=64)
+
+        nc.vector.memset(ws_raw[:].bitcast(I32), 0)
+        nc.vector.memset(xs_raw[:].bitcast(I32), 0)
+        nc.vector.memset(wb_plane[:].bitcast(I32), 0)
+
+        tb_rows = tb.rearrange("(p t) v -> p t v", t=PACK)
+        for u in range(PACK // 2):
+            nc.gpsimd.dma_start(out=tab[u][:], in_=tb_rows[:, 2 * u : 2 * u + 2, :])
+        nc.sync.dma_start(out=w_raw[:].bitcast(I32), in_=w_words.rearrange("z p c -> p z c").bitcast(I32))
+        load_scale_rows(nc.sync, ws_raw, w_scales)
+        nc.sync.dma_start(tok_list[:], offs)
+        for z in range(PASSES):
+            nc.sync.dma_start(out=x_raw[z][:].bitcast(I32), in_=xt_words[z].bitcast(I32))
+        load_scale_rows(nc.sync, xs_raw, xt_scales)
+        nc.sync.dma_start(tab_list[:], offs2)
+        nc.sync.dma_start(
+            out=wb_codes[:].bitcast(I32), in_=wb_words.rearrange("z p n t -> p (z n t)").bitcast(I32)
+        )
+        load_scale_rows(nc.sync, wb_plane, wb_scales)
+        nc.sync.dma_start(out=bias[:], in_=bi[0].partition_broadcast(P))
+
+        w_dealt = sb.tile([P, PACK, PASSES, P], U16, name="w_dealt", align_bytes=64)
+        ws_dealt = sb.tile([P, PACK, PASSES, P], U8, name="ws_dealt", align_bytes=64)
+        nc.vector.tensor_copy(
+            out=w_dealt[:].rearrange("p t z (c i) -> p (z c) t i", i=8),
+            in_=w_raw[:].rearrange("p z (c i t) -> p (z c) t i", i=8, t=PACK),
+        )
+        nc.vector.tensor_copy(
+            out=ws_dealt[:].rearrange("p t z (c i) -> p (z c) t i", i=16),
+            in_=ws_raw[:].rearrange("p z (c i t) -> p (z c) t i", i=16, t=PACK),
+        )
+
+        first = []
+        picked_tab = []
+        for h in range(HALVES):
+            cols = slice(h * LIST_COLS, (h + 1) * LIST_COLS)
+            x_words = sb.tile([P, PASSES, P], U16, name="x_words%d" % h, align_bytes=64)
+            x_plane = sb.tile([P, PASSES, P], U8, name="x_plane%d" % h, align_bytes=64)
+            acc = psum.tile([P, PACK, P], F32, name="first%d" % h)
+            for z in range(PASSES):
+                nc.vector.tensor_copy(out=x_words[:, z, :], in_=x_raw[z][:].indirect(tok_list[:, cols]))
+                nc.vector.tensor_copy(out=x_plane[:, z, :], in_=xs_raw[:, z, :].indirect(tok_list[:, cols]))
+                for t in range(PACK):
+                    nc.tensor.matmul_mx(
+                        out=acc[:, t, :],
+                        lhsT=w_dealt[:, t, z, :].bitcast(FP4X4),
+                        lhsT_scale=ws_dealt[:, t, z, :],
+                        rhs=x_words[:, z, :].bitcast(FP4X4),
+                        rhs_scale=x_plane[:, z, :],
+                        start=(z == 0 and t == 0),
+                        stop=(z == PASSES - 1 and t == PACK - 1),
+                    )
+            first.append(acc)
+            picked = sb.tile([P, PACK, P], F32, name="picked%d" % h, align_bytes=64)
+            for t in range(PACK):
+                nc.scalar.activation(out=picked[:, t, :], in_=tab[t // 2][:, t % 2, :].indirect(tab_list[:, cols]), func=ACT.Copy)
+            picked_tab.append(picked)
+
+        second = []
+        for h in range(HALVES):
+            diff = sb.tile([P, P, PACK], BF16, name="diff%d" % h, align_bytes=64)
+            nc.vector.tensor_tensor(
+                out=diff[:].rearrange("p (c i) t -> p c t i", i=4),
+                in0=first[h][:].rearrange("p t (c i) -> p c t i", i=4),
+                in1=picked_tab[h][:].rearrange("p t (c i) -> p c t i", i=4),
+                op=ALU.subtract,
+            )
+            hid = sb.tile([P, P * PACK], BF16, name="hid%d" % h, align_bytes=64)
+            nc.vector.tensor_scalar_max(out=hid[:], in0=diff[:].rearrange("p j t -> p (j t)"), scalar1=0.0)
+            hid_codes = sb.tile([P, P], U32, name="hid_codes%d" % h, align_bytes=64)
+            hid_plane = sb.tile([P, P], U8, name="hid_plane%d" % h, align_bytes=64)
+            nc.vector.quantize_mx(out=hid_codes[:].bitcast(E5M2X4), scales=hid_plane[:], in_=hid[:])
+            acc2 = psum.tile([P, N], F32, name="second%d" % h)
+            nc.tensor.matmul_mx(
+                out=acc2[:],
+                lhsT=hid_codes[:].bitcast(E5M2X4),
+                lhsT_scale=hid_plane[:],
+                rhs=wb_codes[:].bitcast(E5M2X4),
+                rhs_scale=wb_plane[:, 0, :],
+                start=True,
+                stop=True,
+            )
+            second.append(acc2)
+
+        for h in range(HALVES):
+            neg_logit = sb.tile([P, N], F32, name="neg_logit%d" % h, align_bytes=64)
+            nc.vector.scalar_tensor_tensor(
+                out=neg_logit[:], in0=second[h][:], scalar=-0.7, in1=bias[:], op0=ALU.mult, op1=ALU.subtract
+            )
+            neg_max = sb.tile([P, 1], F32, name="neg_max%d" % h)
+            nc.vector.tensor_reduce(out=neg_max[:], in_=neg_logit[:], axis=AXIS.X, op=ALU.min)
+            expd = sb.tile([P, N], F32, name="expd%d" % h, align_bytes=64)
+            total = sb.tile([P, 1], F32, name="total%d" % h)
+            nc.scalar.activation(
+                out=expd[:], in_=neg_logit[:], func=ACT.Exp, bias=neg_max[:], scale=-1.0, accum_out=total[:]
+            )
+            inv = sb.tile([P, 1], F32, name="inv%d" % h)
+            nc.vector.reciprocal(out=inv[:], in_=total[:])
+            shares = sb.tile([P, N], F32, name="shares%d" % h, align_bytes=64)
+            nc.vector.tensor_scalar(
+                out=shares[:], in0=expd[:], scalar1=inv[:], scalar2=256.0, op0=ALU.mult, op1=ALU.mult
+            )
+            nc.sync.dma_start(out=out[h * P : (h + 1) * P, :], in_=shares[:])

@@ -54,6 +54,11 @@ def tile_list_picked_overtable_rowshares_kernel(
         wb_plane = sb.tile([P, 1, N], U8, name="wb_plane", align_bytes=64)
         bias = sb.tile([P, N], F32, name="bias", align_bytes=64)
 
+        warm_in = sb.tile([P, 1], F32, name="warm_in")
+        warm_out = sb.tile([P, 1], F32, name="warm_out")
+        nc.gpsimd.memset(warm_in[:], 0.0)
+        nc.scalar.activation(out=warm_out[:], in_=warm_in[:], func=ACT.Exp)
+
         nc.vector.memset(ws_raw[:].bitcast(I32), 0)
         nc.vector.memset(xs_raw[:].bitcast(I32), 0)
         nc.vector.memset(wb_plane[:].bitcast(I32), 0)

@@ -1,6 +1,7 @@
 from contextlib import ExitStack
 
 import concourse.mybir as mybir
+from concourse.masks import make_identity
 
 K, T, J, R, V, N = 1024, 1024, 256, 512, 512, 256
 FLOPS = 2 * K * R * J + 2 * R * J * N
@@ -49,7 +50,9 @@ def tile_list_picked_overtable_rowshares_kernel(
         ws_raw = sb.tile([P, PASSES, R], U8, name="ws_raw", align_bytes=64)
         x_raw = [sb.tile([P, T], U16, name="x_raw%d" % z, align_bytes=64) for z in range(PASSES)]
         xs_raw = sb.tile([P, PASSES, T], U8, name="xs_raw", align_bytes=64)
-        tab = [sb.tile([P, 2, V], F32, name="tab%d" % u, align_bytes=64) for u in range(PACK // 2)]
+        tab01 = sb.tile([P, 2, V], F32, name="tab01", align_bytes=64)
+        tab23 = sb.tile([P, 2, V], F32, name="tab23", align_bytes=64)
+        tab = [tab01[:, 0, :], tab01[:, 1, :], tab23[:, 0, :], tab23[:, 1, :]]
         wb_codes = sb.tile([P, N], U32, name="wb_codes", align_bytes=64)
         wb_plane = sb.tile([P, 1, N], U8, name="wb_plane", align_bytes=64)
         bias = sb.tile([P, N], F32, name="bias", align_bytes=64)
@@ -64,20 +67,25 @@ def tile_list_picked_overtable_rowshares_kernel(
         nc.vector.memset(wb_plane[:].bitcast(I32), 0)
 
         tb_rows = tb.rearrange("(p t) v -> p t v", t=PACK)
-        for u in range(PACK // 2):
-            nc.gpsimd.dma_start(out=tab[u][:], in_=tb_rows[:, 2 * u : 2 * u + 2, :])
+        nc.gpsimd.dma_start(out=tab01[:], in_=tb_rows[:, 0 : 2, :])
+        nc.gpsimd.dma_start(out=tab23[:], in_=tb_rows[:, 2 : 4, :])
+        nc.sync.dma_start(tok_list[:], offs)
         nc.sync.dma_start(out=w_raw[:].bitcast(I32), in_=w_words.rearrange("z p c -> p z c").bitcast(I32))
         load_scale_rows(nc.sync, ws_raw, w_scales)
-        nc.sync.dma_start(tok_list[:], offs)
-        for z in range(PASSES):
-            nc.sync.dma_start(out=x_raw[z][:].bitcast(I32), in_=xt_words[z].bitcast(I32))
+        nc.sync.dma_start(out=x_raw[0][:].bitcast(I32), in_=xt_words[0].bitcast(I32))
+        nc.sync.dma_start(out=x_raw[1][:].bitcast(I32), in_=xt_words[1].bitcast(I32))
         load_scale_rows(nc.sync, xs_raw, xt_scales)
         nc.sync.dma_start(tab_list[:], offs2)
-        nc.sync.dma_start(
-            out=wb_codes[:].bitcast(I32), in_=wb_words.rearrange("z p n t -> p (z n t)").bitcast(I32)
-        )
+        ident = sb.tile([P, P], F32, name="ident", align_bytes=64)
+        make_identity(nc, ident[:])
+        bias_cols = sb.tile([P, N // P], F32, name="bias_cols", align_bytes=64)
+        nc.sync.dma_start(out=bias_cols[:], in_=bi[0].rearrange("(p c) -> p c", p=P))
+        bias_spread = psum.tile([P, N // P, P], F32, name="bias_spread")
+        for c in range(N // P):
+            nc.tensor.transpose(bias_spread[:, c, :], bias_cols[:, c : c + 1].to_broadcast([P, P]), ident[:])
+        nc.scalar.copy(out=bias[:].rearrange("p (q c) -> p q c", c=N // P), in_=bias_spread[:].rearrange("p c q -> p q c"))
+        nc.sync.dma_start(out=wb_codes[:].bitcast(I32), in_=wb_words.rearrange("z p n t -> p (z n t)").bitcast(I32))
         load_scale_rows(nc.sync, wb_plane, wb_scales)
-        nc.sync.dma_start(out=bias[:], in_=bi[0].partition_broadcast(P))
 
         w_dealt = sb.tile([P, PACK, PASSES, P], U16, name="w_dealt", align_bytes=64)
         ws_dealt = sb.tile([P, PACK, PASSES, P], U8, name="ws_dealt", align_bytes=64)
@@ -90,22 +98,24 @@ def tile_list_picked_overtable_rowshares_kernel(
             in_=ws_raw[:].rearrange("p z (c i t) -> p (z c) t i", i=16, t=PACK),
         )
 
+        x_words = sb.tile([P, PASSES, J], U16, name="x_words", align_bytes=64)
+        for z in range(PASSES):
+            nc.vector.tensor_copy(out=x_words[:, z, :], in_=x_raw[z][:].indirect(tok_list[:]))
+
         first = []
         picked_tab = []
         for h in range(HALVES):
             cols = slice(h * LIST_COLS, (h + 1) * LIST_COLS)
-            x_words = sb.tile([P, PASSES, P], U16, name="x_words%d" % h, align_bytes=64)
             x_plane = sb.tile([P, PASSES, P], U8, name="x_plane%d" % h, align_bytes=64)
             acc = psum.tile([P, PACK, P], F32, name="first%d" % h)
             for z in range(PASSES):
-                nc.vector.tensor_copy(out=x_words[:, z, :], in_=x_raw[z][:].indirect(tok_list[:, cols]))
                 nc.vector.tensor_copy(out=x_plane[:, z, :], in_=xs_raw[:, z, :].indirect(tok_list[:, cols]))
                 for t in range(PACK):
                     nc.tensor.matmul_mx(
                         out=acc[:, t, :],
                         lhsT=w_dealt[:, t, z, :].bitcast(FP4X4),
                         lhsT_scale=ws_dealt[:, t, z, :],
-                        rhs=x_words[:, z, :].bitcast(FP4X4),
+                        rhs=x_words[:, z, h * P : (h + 1) * P].bitcast(FP4X4),
                         rhs_scale=x_plane[:, z, :],
                         start=(z == 0 and t == 0),
                         stop=(z == PASSES - 1 and t == PACK - 1),
@@ -113,7 +123,7 @@ def tile_list_picked_overtable_rowshares_kernel(
             first.append(acc)
             picked = sb.tile([P, PACK, P], F32, name="picked%d" % h, align_bytes=64)
             for t in range(PACK):
-                nc.scalar.activation(out=picked[:, t, :], in_=tab[t // 2][:, t % 2, :].indirect(tab_list[:, cols]), func=ACT.Copy)
+                nc.scalar.activation(out=picked[:, t, :], in_=tab[t].indirect(tab_list[:, cols]), func=ACT.Copy)
             picked_tab.append(picked)
 
         second = []

@@ -50,9 +50,11 @@ def tile_list_picked_overtable_rowshares_kernel(
         ws_raw = sb.tile([P, PASSES, R], U8, name="ws_raw", align_bytes=64)
         x_raw = [sb.tile([P, T], U16, name="x_raw%d" % z, align_bytes=64) for z in range(PASSES)]
         xs_raw = sb.tile([P, PASSES, T], U8, name="xs_raw", align_bytes=64)
-        tab01 = sb.tile([P, 2, V], F32, name="tab01", align_bytes=64)
-        tab23 = sb.tile([P, 2, V], F32, name="tab23", align_bytes=64)
-        tab = [tab01[:, 0, :], tab01[:, 1, :], tab23[:, 0, :], tab23[:, 1, :]]
+        tab0 = sb.tile([P, 1, V], F32, name="tab0", align_bytes=64)
+        tab1 = sb.tile([P, 1, V], F32, name="tab1", align_bytes=64)
+        tab2 = sb.tile([P, 1, V], F32, name="tab2", align_bytes=64)
+        tab3 = sb.tile([P, 1, V], F32, name="tab3", align_bytes=64)
+        tab = [tab0[:, 0, :], tab1[:, 0, :], tab2[:, 0, :], tab3[:, 0, :]]
         wb_codes = sb.tile([P, N], U32, name="wb_codes", align_bytes=64)
         wb_plane = sb.tile([P, 1, N], U8, name="wb_plane", align_bytes=64)
         bias = sb.tile([P, N], F32, name="bias", align_bytes=64)
@@ -67,23 +69,25 @@ def tile_list_picked_overtable_rowshares_kernel(
         nc.vector.memset(wb_plane[:].bitcast(I32), 0)
 
         tb_rows = tb.rearrange("(p t) v -> p t v", t=PACK)
-        nc.gpsimd.dma_start(out=tab01[:], in_=tb_rows[:, 0 : 2, :])
-        nc.gpsimd.dma_start(out=tab23[:], in_=tb_rows[:, 2 : 4, :])
-        nc.sync.dma_start(tok_list[:], offs)
-        nc.sync.dma_start(out=w_raw[:].bitcast(I32), in_=w_words.rearrange("z p c -> p z c").bitcast(I32))
-        load_scale_rows(nc.sync, ws_raw, w_scales)
-        nc.sync.dma_start(out=x_raw[0][:].bitcast(I32), in_=xt_words[0].bitcast(I32))
-        nc.sync.dma_start(out=x_raw[1][:].bitcast(I32), in_=xt_words[1].bitcast(I32))
-        load_scale_rows(nc.sync, xs_raw, xt_scales)
-        nc.sync.dma_start(tab_list[:], offs2)
         ident = sb.tile([P, P], F32, name="ident", align_bytes=64)
         make_identity(nc, ident[:])
         bias_cols = sb.tile([P, N // P], F32, name="bias_cols", align_bytes=64)
-        nc.sync.dma_start(out=bias_cols[:], in_=bi[0].rearrange("(p c) -> p c", p=P))
+        nc.gpsimd.dma_start(out=bias_cols[:], in_=bi[0].rearrange("(p c) -> p c", p=P))
         bias_spread = psum.tile([P, N // P, P], F32, name="bias_spread")
         for c in range(N // P):
             nc.tensor.transpose(bias_spread[:, c, :], bias_cols[:, c : c + 1].to_broadcast([P, P]), ident[:])
         nc.scalar.copy(out=bias[:].rearrange("p (q c) -> p q c", c=N // P), in_=bias_spread[:].rearrange("p c q -> p q c"))
+        nc.sync.dma_start(tok_list[:], offs)
+        nc.sync.dma_start(tab_list[:], offs2)
+        nc.sync.dma_start(out=w_raw[:].bitcast(I32), in_=w_words.rearrange("z p c -> p z c").bitcast(I32))
+        load_scale_rows(nc.sync, ws_raw, w_scales)
+        nc.sync.dma_start(out=x_raw[0][:].bitcast(I32), in_=xt_words[0].bitcast(I32))
+        nc.sync.dma_start(out=x_raw[1][:].bitcast(I32), in_=xt_words[1].bitcast(I32))
+        nc.sync.dma_start(out=tab0[:], in_=tb_rows[:, 0 : 1, :])
+        load_scale_rows(nc.sync, xs_raw, xt_scales)
+        nc.sync.dma_start(out=tab1[:], in_=tb_rows[:, 1 : 2, :])
+        nc.sync.dma_start(out=tab2[:], in_=tb_rows[:, 2 : 3, :])
+        nc.sync.dma_start(out=tab3[:], in_=tb_rows[:, 3 : 4, :])
         nc.sync.dma_start(out=wb_codes[:].bitcast(I32), in_=wb_words.rearrange("z p n t -> p (z n t)").bitcast(I32))
         load_scale_rows(nc.sync, wb_plane, wb_scales)
 
@@ -128,15 +132,14 @@ def tile_list_picked_overtable_rowshares_kernel(
 
         second = []
         for h in range(HALVES):
-            diff = sb.tile([P, P, PACK], BF16, name="diff%d" % h, align_bytes=64)
-            nc.vector.tensor_tensor(
-                out=diff[:].rearrange("p (c i) t -> p c t i", i=4),
-                in0=first[h][:].rearrange("p t (c i) -> p c t i", i=4),
-                in1=picked_tab[h][:].rearrange("p t (c i) -> p c t i", i=4),
-                op=ALU.subtract,
-            )
+            diff = sb.tile([P, PACK, P], BF16, name="diff%d" % h, align_bytes=64)
+            nc.vector.tensor_tensor(out=diff[:], in0=first[h][:], in1=picked_tab[h][:], op=ALU.subtract)
             hid = sb.tile([P, P * PACK], BF16, name="hid%d" % h, align_bytes=64)
-            nc.vector.tensor_scalar_max(out=hid[:], in0=diff[:].rearrange("p j t -> p (j t)"), scalar1=0.0)
+            nc.vector.tensor_scalar_max(
+                out=hid[:].rearrange("p (c i t) -> p c t i", i=4, t=PACK),
+                in0=diff[:].rearrange("p t (c i) -> p c t i", i=4),
+                scalar1=0.0,
+            )
             hid_codes = sb.tile([P, P], U32, name="hid_codes%d" % h, align_bytes=64)
             hid_plane = sb.tile([P, P], U8, name="hid_plane%d" % h, align_bytes=64)
             nc.vector.quantize_mx(out=hid_codes[:].bitcast(E5M2X4), scales=hid_plane[:], in_=hid[:])

from contextlib import ExitStack

import concourse.mybir as mybir
from concourse.masks import make_identity

K, T, J, R, V, N = 1024, 1024, 256, 512, 512, 256
FLOPS = 2 * K * R * J + 2 * R * J * N

F32 = mybir.dt.float32
BF16 = mybir.dt.bfloat16
I32 = mybir.dt.int32
U32 = mybir.dt.uint32
U16 = mybir.dt.uint16
U8 = mybir.dt.uint8
FP4X4 = mybir.dt.float4_e2m1fn_x4
E5M2X4 = mybir.dt.float8_e5m2_x4
ALU = mybir.AluOpType
ACT = mybir.ActivationFunctionType
AXIS = mybir.AxisListType

P = 128
PACK = 4
PASSES = K // (P * PACK)
QUADS = 4
HALVES = J // P
LIST_COLS = P // 16


def load_scale_rows(queue, plane, scales):
    for q in range(QUADS):
        queue.dma_start(
            out=plane[32 * q : 32 * q + 4, :, :].bitcast(I32),
            in_=scales[:, 4 * q : 4 * q + 4, :].rearrange("z r c -> r z c").bitcast(I32),
        )


def tile_list_picked_overtable_rowshares_kernel(
    tc, xt_words, xt_scales, w_words, w_scales, tb, wb_words, wb_scales, bi, offs, offs2, out
):
    nc = tc.nc
    with ExitStack() as ctx:
        lists = ctx.enter_context(tc.tile_pool(name="lists", bufs=1))
        sb = ctx.enter_context(tc.tile_pool(name="sb", bufs=1))
        psum = ctx.enter_context(tc.psum_pool(name="psum", bufs=1))

        tok_list = lists.tile([P, J // 16], U16, name="tok_list")
        tab_list = lists.tile([P, J // 16], U16, name="tab_list")

        w_raw = sb.tile([P, PASSES, R], U16, name="w_raw", align_bytes=64)
        ws_raw = sb.tile([P, PASSES, R], U8, name="ws_raw", align_bytes=64)
        x_raw = [sb.tile([P, T], U16, name="x_raw%d" % z, align_bytes=64) for z in range(PASSES)]
        xs_raw = sb.tile([P, PASSES, T], U8, name="xs_raw", align_bytes=64)
        tab0 = sb.tile([P, 1, V], F32, name="tab0", align_bytes=64)
        tab1 = sb.tile([P, 1, V], F32, name="tab1", align_bytes=64)
        tab2 = sb.tile([P, 1, V], F32, name="tab2", align_bytes=64)
        tab3 = sb.tile([P, 1, V], F32, name="tab3", align_bytes=64)
        tab = [tab0[:, 0, :], tab1[:, 0, :], tab2[:, 0, :], tab3[:, 0, :]]
        wb_codes = sb.tile([P, N], U32, name="wb_codes", align_bytes=64)
        wb_plane = sb.tile([P, 1, N], U8, name="wb_plane", align_bytes=64)
        bias = sb.tile([P, N], F32, name="bias", align_bytes=64)

        warm_in = sb.tile([P, 1], F32, name="warm_in")
        warm_out = sb.tile([P, 1], F32, name="warm_out")
        nc.gpsimd.memset(warm_in[:], 0.0)
        nc.scalar.activation(out=warm_out[:], in_=warm_in[:], func=ACT.Exp)

        nc.vector.memset(ws_raw[:].bitcast(I32), 0)
        nc.vector.memset(xs_raw[:].bitcast(I32), 0)
        nc.vector.memset(wb_plane[:].bitcast(I32), 0)

        tb_rows = tb.rearrange("(p t) v -> p t v", t=PACK)
        ident = sb.tile([P, P], F32, name="ident", align_bytes=64)
        make_identity(nc, ident[:])
        bias_cols = sb.tile([P, N // P], F32, name="bias_cols", align_bytes=64)
        nc.gpsimd.dma_start(out=bias_cols[:], in_=bi[0].rearrange("(p c) -> p c", p=P))
        bias_spread = psum.tile([P, N // P, P], F32, name="bias_spread")
        for c in range(N // P):
            nc.tensor.transpose(bias_spread[:, c, :], bias_cols[:, c : c + 1].to_broadcast([P, P]), ident[:])
        nc.scalar.copy(out=bias[:].rearrange("p (q c) -> p q c", c=N // P), in_=bias_spread[:].rearrange("p c q -> p q c"))
        nc.sync.dma_start(tok_list[:], offs)
        nc.sync.dma_start(tab_list[:], offs2)
        nc.sync.dma_start(out=w_raw[:].bitcast(I32), in_=w_words.rearrange("z p c -> p z c").bitcast(I32))
        load_scale_rows(nc.sync, ws_raw, w_scales)
        nc.sync.dma_start(out=x_raw[0][:].bitcast(I32), in_=xt_words[0].bitcast(I32))
        nc.sync.dma_start(out=x_raw[1][:].bitcast(I32), in_=xt_words[1].bitcast(I32))
        nc.sync.dma_start(out=tab0[:], in_=tb_rows[:, 0 : 1, :])
        load_scale_rows(nc.sync, xs_raw, xt_scales)
        nc.sync.dma_start(out=tab1[:], in_=tb_rows[:, 1 : 2, :])
        nc.sync.dma_start(out=tab2[:], in_=tb_rows[:, 2 : 3, :])
        nc.sync.dma_start(out=tab3[:], in_=tb_rows[:, 3 : 4, :])
        nc.sync.dma_start(out=wb_codes[:].bitcast(I32), in_=wb_words.rearrange("z p n t -> p (z n t)").bitcast(I32))
        load_scale_rows(nc.sync, wb_plane, wb_scales)

        w_dealt = sb.tile([P, PACK, PASSES, P], U16, name="w_dealt", align_bytes=64)
        ws_dealt = sb.tile([P, PACK, PASSES, P], U8, name="ws_dealt", align_bytes=64)
        nc.vector.tensor_copy(
            out=w_dealt[:].rearrange("p t z (c i) -> p (z c) t i", i=8),
            in_=w_raw[:].rearrange("p z (c i t) -> p (z c) t i", i=8, t=PACK),
        )
        nc.vector.tensor_copy(
            out=ws_dealt[:].rearrange("p t z (c i) -> p (z c) t i", i=16),
            in_=ws_raw[:].rearrange("p z (c i t) -> p (z c) t i", i=16, t=PACK),
        )

        x_words = sb.tile([P, PASSES, J], U16, name="x_words", align_bytes=64)
        for z in range(PASSES):
            nc.vector.tensor_copy(out=x_words[:, z, :], in_=x_raw[z][:].indirect(tok_list[:]))

        first = []
        picked_tab = []
        for h in range(HALVES):
            cols = slice(h * LIST_COLS, (h + 1) * LIST_COLS)
            x_plane = sb.tile([P, PASSES, P], U8, name="x_plane%d" % h, align_bytes=64)
            acc = psum.tile([P, PACK, P], F32, name="first%d" % h)
            for z in range(PASSES):
                nc.vector.tensor_copy(out=x_plane[:, z, :], in_=xs_raw[:, z, :].indirect(tok_list[:, cols]))
                for t in range(PACK):
                    nc.tensor.matmul_mx(
                        out=acc[:, t, :],
                        lhsT=w_dealt[:, t, z, :].bitcast(FP4X4),
                        lhsT_scale=ws_dealt[:, t, z, :],
                        rhs=x_words[:, z, h * P : (h + 1) * P].bitcast(FP4X4),
                        rhs_scale=x_plane[:, z, :],
                        start=(z == 0 and t == 0),
                        stop=(z == PASSES - 1 and t == PACK - 1),
                    )
            first.append(acc)
            picked = sb.tile([P, PACK, P], F32, name="picked%d" % h, align_bytes=64)
            for t in range(PACK):
                nc.scalar.activation(out=picked[:, t, :], in_=tab[t].indirect(tab_list[:, cols]), func=ACT.Copy)
            picked_tab.append(picked)

        second = []
        for h in range(HALVES):
            diff = sb.tile([P, PACK, P], BF16, name="diff%d" % h, align_bytes=64)
            nc.vector.tensor_tensor(out=diff[:], in0=first[h][:], in1=picked_tab[h][:], op=ALU.subtract)
            hid = sb.tile([P, P * PACK], BF16, name="hid%d" % h, align_bytes=64)
            nc.vector.tensor_scalar_max(
                out=hid[:].rearrange("p (c i t) -> p c t i", i=4, t=PACK),
                in0=diff[:].rearrange("p t (c i) -> p c t i", i=4),
                scalar1=0.0,
            )
            hid_codes = sb.tile([P, P], U32, name="hid_codes%d" % h, align_bytes=64)
            hid_plane = sb.tile([P, P], U8, name="hid_plane%d" % h, align_bytes=64)
            nc.vector.quantize_mx(out=hid_codes[:].bitcast(E5M2X4), scales=hid_plane[:], in_=hid[:])
            acc2 = psum.tile([P, N], F32, name="second%d" % h)
            nc.tensor.matmul_mx(
                out=acc2[:],
                lhsT=hid_codes[:].bitcast(E5M2X4),
                lhsT_scale=hid_plane[:],
                rhs=wb_codes[:].bitcast(E5M2X4),
                rhs_scale=wb_plane[:, 0, :],
                start=True,
                stop=True,
            )
            second.append(acc2)

        for h in range(HALVES):
            neg_logit = sb.tile([P, N], F32, name="neg_logit%d" % h, align_bytes=64)
            nc.vector.scalar_tensor_tensor(
                out=neg_logit[:], in0=second[h][:], scalar=-0.7, in1=bias[:], op0=ALU.mult, op1=ALU.subtract
            )
            neg_max = sb.tile([P, 1], F32, name="neg_max%d" % h)
            nc.vector.tensor_reduce(out=neg_max[:], in_=neg_logit[:], axis=AXIS.X, op=ALU.min)
            expd = sb.tile([P, N], F32, name="expd%d" % h, align_bytes=64)
            total = sb.tile([P, 1], F32, name="total%d" % h)
            nc.scalar.activation(
                out=expd[:], in_=neg_logit[:], func=ACT.Exp, bias=neg_max[:], scale=-1.0, accum_out=total[:]
            )
            inv = sb.tile([P, 1], F32, name="inv%d" % h)
            nc.vector.reciprocal(out=inv[:], in_=total[:])
            shares = sb.tile([P, N], F32, name="shares%d" % h, align_bytes=64)
            nc.vector.tensor_scalar(
                out=shares[:], in0=expd[:], scalar1=inv[:], scalar2=256.0, op0=ALU.mult, op1=ALU.mult
            )
            nc.sync.dma_start(out=out[h * P : (h + 1) * P, :], in_=shares[:])
